import numpy as np
import ml_dtypes


def mxq(x, axis, fmt="e4m3"):
    dtype, down = {"e4m3": (ml_dtypes.float8_e4m3fn, 7), "e5m2": (ml_dtypes.float8_e5m2, 14)}[fmt]
    v = np.moveaxis(np.asarray(x, np.float32).astype(ml_dtypes.bfloat16).astype(np.float64), axis, -1)
    blocks = v.reshape(v.shape[:-1] + (-1, 32))
    amax = np.abs(blocks).max(-1, keepdims=True)
    byte = np.maximum(np.where(amax > 0, np.frexp(amax)[1] - 1 + 127, 0) - down, 1)
    scale = np.exp2(byte - 127.0)
    codes = (blocks / scale).astype(np.float32).astype(dtype).astype(np.float64)
    return np.moveaxis((codes * scale).reshape(v.shape), -1, axis)


WIDE = False


def mx_kscale(k, group=512):
    if not WIDE:
        return np.ones(k)
    levels = np.array([10, -10, 5, -5, 0])
    if group != 512:
        return np.exp2(np.random.permutation(np.resize(levels, k // group))).repeat(group)
    if k % 512:
        return np.exp2(np.random.permutation(np.resize(levels, k // 32))).repeat(32)
    a = np.empty((k // 512, 16))
    for p in range(k // 512):
        a[p, :8] = np.random.permutation(np.resize(levels, 8))
        for g in range(8):
            far = levels[np.abs(levels - a[p, g]) >= 10]
            a[p, g + 8] = far[np.random.randint(len(far))]
    return np.exp2(a.ravel()).repeat(32)


def f64(x):
    return np.asarray(x).astype(np.float64)


def striped(idx):
    return np.tile(np.asarray(idx).reshape(-1, 16).T, (8, 1)).astype(np.uint16)


def unstriped(offs):
    return offs[:16].T.reshape(-1).astype(np.int64)


H, KV, D, NQ, N = 2, 2, 256, 512, 1024


def setup_inputs():
    n = np.random.standard_normal
    s = mx_kscale(D, 0)[:, None]
    u = mx_kscale(N)
    t = np.random.uniform(0.5, 2.0, N) * u
    v = n((KV, N, 128))
    v[:, :, 127] = 1.0
    return {
        "qT": (n((H, D, NQ)) * s * (0.70 / np.sqrt(D))).astype(np.float32),
        "kT": (n((KV, D, N)) / s).astype(np.float32),
        "t": t.reshape(N, 1).astype(np.float32),
        "v": (v / t[:, None]).astype(np.float32),
        "kb": (0.5 * n((N, 1))).astype(np.float32),
        "mask": (np.arange(N)[:, None] <= np.sort(np.random.randint(N // 4, N, NQ))[None, :]).astype(np.float32),
        "sink": (N * np.random.uniform(0.1, 1.0, (H, NQ, 1))).astype(np.float32),
    }


def reference(qT, kT, t, v, kb, mask, sink):
    a = mxq(f64(kT), 1, "e4m3").transpose(0, 2, 1) @ mxq(f64(qT), 1, "e4m3")
    a = a + f64(kb)
    p = np.exp(a)
    p = p * f64(mask)
    w = p * f64(t)
    y = mxq(w, 1, "e4m3").transpose(0, 2, 1) @ mxq(f64(v), 1, "e4m3")
    y = y / (y[:, :, 127:128] + f64(sink))
    return y

@@ -1,0 +1,258 @@
+from contextlib import ExitStack
+
+import concourse.mybir as mybir
+
+H, D, NQ, N, E = 2, 256, 512, 1024, 128
+FLOPS = 2 * H * NQ * N * (D + E)
+
+F32 = mybir.dt.float32
+BF16 = mybir.dt.bfloat16
+U32 = mybir.dt.uint32
+U8 = mybir.dt.uint8
+FP8X4 = mybir.dt.float8_e4m3fn_x4
+ACT = mybir.ActivationFunctionType
+ALU = mybir.AluOpType
+
+P = 128
+PACK = 4
+PASS = P * PACK
+PASSES = N // PASS
+ROWS = D // PACK
+QB = 128
+HALF = NQ // 2
+K_SPLIT = 84
+Q_SPLIT = 42
+
+
+def tile_rows_a_exp_kb_mask_sink_kernel(tc, qT, kT, t, v, kb, mask, sink, out):
+    nc = tc.nc
+    with ExitStack() as ctx:
+        keep = ctx.enter_context(tc.tile_pool(name="keep", bufs=1))
+        score_pools = [ctx.enter_context(tc.psum_pool(name="scores%d" % h, bufs=3)) for h in range(H)]
+        y_pool = ctx.enter_context(tc.psum_pool(name="y", bufs=2))
+        ctx.enter_context(tc.manual_schedule())
+
+        def sb(name, shape, dtype):
+            return keep.tile(shape, dtype, name=name, align_bytes=64)
+
+        def operand(name, words):
+            return (sb(name + "_bf", [P, PACK * words], BF16), sb(name + "_codes", [P, words], U32), sb(name + "_scales", [P, words], U8))
+
+        def quantise(op, c0, c1):
+            values, codes, scales = op
+            nc.vector.quantize_mx(out=codes[:, c0:c1].bitcast(FP8X4), scales=scales[:, c0:c1], in_=values[:, PACK * c0 : PACK * c1])
+
+        warm_in = sb("warm_in", [P, 1], F32)
+        warm_out = sb("warm_out", [P, 1], F32)
+        kb_sb = sb("kb_sb", [P, PASSES, PACK], F32)
+        t_sb = sb("t_sb", [P, PASSES, PACK], F32)
+        sink_sb = sb("sink_sb", [P, H * NQ // QB], F32)
+        k_raw = [sb("k_raw%d" % g, [P, PACK, PASS], F32) for g in range(PASSES)]
+        q_raw = sb("q_raw", [P, PACK, NQ], F32)
+        mask_raw = [[sb("mask_raw%d_%d" % (g, u), [P, 2, NQ], F32) for u in range(2)] for g in range(PASSES)]
+        v_raw = [sb("v_raw%d" % h, [P, PASSES, PACK, E], F32) for h in range(H)]
+        mt = [sb("mt%d" % g, [P, PACK, NQ], F32) for g in range(PASSES)]
+        k_op = [operand("k%d" % g, PASS) for g in range(PASSES)]
+        q_op = [operand("q%d" % u, HALF) for u in range(2)]
+        v_op = [operand("v%d" % h, PASSES * E) for h in range(H)]
+        w_op = {(h, g): operand("w%d_%d" % (h, g), NQ) for h in range(H) for g in range(PASSES)}
+        p_sb = {(h, g): sb("p%d_%d" % (h, g), [P, PACK, NQ], F32) for h in range(H) for g in range(PASSES)}
+        den = sb("den", [P, H * NQ // QB], F32)
+        inv = sb("inv", [P, H * NQ // QB], F32)
+
+        k_rows = kT.rearrange("h (p j) n -> (h p) j n", j=PACK)
+        mask_rows = mask.rearrange("(g p j) q -> g p j q", g=PASSES, j=PACK)
+        nc.vector.memset(warm_in[:], 0.0)
+        nc.scalar.dma_start(out=kb_sb[:], in_=kb.rearrange("(g p j) o -> p g (j o)", g=PASSES, j=PACK))
+        nc.scalar.dma_start(out=t_sb[:], in_=t.rearrange("(g p j) o -> p g (j o)", g=PASSES, j=PACK))
+        nc.scalar.activation(out=warm_out[:], in_=warm_in[:], func=ACT.Exp)
+        nc.sync.dma_start(out=k_raw[0][:], in_=k_rows[:, :, 0:PASS])
+        nc.sync.dma_start(out=q_raw[:], in_=qT.rearrange("h (p j) n -> (h p) j n", j=PACK))
+        for u in range(2):
+            nc.sync.dma_start(out=mask_raw[0][u][:], in_=mask_rows[0, :, 2 * u : 2 * u + 2, :])
+        nc.sync.dma_start(out=k_raw[1][:], in_=k_rows[:, :, PASS:N])
+        for u in range(2):
+            nc.sync.dma_start(out=mask_raw[1][u][:], in_=mask_rows[1, :, 2 * u : 2 * u + 2, :])
+        for h in range(H):
+            nc.sync.dma_start(out=v_raw[h][:].rearrange("p g j e -> p g (j e)"), in_=v[h].rearrange("(g p j) e -> p g (j e)", g=PASSES, j=PACK))
+        with nc.allow_non_contiguous_dma(reason="one sink value a partition"):
+            nc.sync.dma_start(out=sink_sb[:].unsqueeze(2), in_=sink.rearrange("h (b p) o -> p (h b) o", p=P))
+
+        def copy_on(engine, dst, src):
+            if engine == "vector":
+                nc.vector.tensor_copy(out=dst, in_=src)
+            else:
+                nc.scalar.copy(out=dst, in_=src)
+
+        def round_k(g, engine, s0, s1):
+            dst = k_op[g][0][:].rearrange("p (r s j) -> p s j r", r=PACK, j=PACK)
+            src = k_raw[g][:].rearrange("p j (s r) -> p s j r", r=PACK)
+            copy_on(engine, dst[:, s0:s1], src[:, s0:s1])
+
+        def round_q(u, engine, c0, c1):
+            dst = q_op[u][0][:].rearrange("p (c i j) -> p c j i", i=4, j=PACK)
+            src = q_raw[:, :, u * HALF : (u + 1) * HALF].rearrange("p j (c i) -> p c j i", i=4)
+            copy_on(engine, dst[:, c0:c1], src[:, c0:c1])
+
+        def round_v(h):
+            dst = v_op[h][0][:].rearrange("p (g c i j) -> p g c j i", g=PASSES, i=4, j=PACK)
+            src = v_raw[h][:].rearrange("p g j (c i) -> p g c j i", i=4)
+            nc.scalar.copy(out=dst, in_=src)
+
+        def mask_times_t(g, j, engine):
+            if engine == "vector":
+                nc.vector.tensor_scalar(out=mt[g][:, j, :], in0=mask_raw[g][j // 2][:, j % 2, :], scalar1=t_sb[:, g, j : j + 1], scalar2=None, op0=ALU.mult)
+            else:
+                nc.scalar.activation(out=mt[g][:, j, :], in_=mask_raw[g][j // 2][:, j % 2, :], func=ACT.Copy, scale=t_sb[:, g, j : j + 1])
+
+        jobs = []
+        for u in range(2):
+            for j0 in (0, 2):
+                jobs.append((0, 0, [(j0, u * HALF, HALF), (j0 + 1, u * HALF, HALF)]))
+        for h, g in ((1, 0), (0, 1), (1, 1)):
+            for j in range(PACK):
+                jobs.append((h, g, [(j, 0, NQ)]))
+        banks = {}
+
+        def scores(n):
+            if n >= len(jobs):
+                return
+            h, g, parts = jobs[n]
+            bank = score_pools[h].tile([P, NQ], F32, name="bank")
+            banks[n] = bank
+            rows = slice(h * ROWS, (h + 1) * ROWS)
+            at = 0
+            for j, q0, width in parts:
+                for q in range(q0, q0 + width, QB):
+                    u, c = divmod(q, HALF)
+                    nc.tensor.matmul_mx(
+                        out=bank[:, at : at + QB],
+                        lhsT=k_op[g][1][rows, j * P : (j + 1) * P].bitcast(FP8X4),
+                        lhsT_scale=k_op[g][2][rows, j * P : (j + 1) * P],
+                        rhs=q_op[u][1][rows, c : c + QB].bitcast(FP8X4),
+                        rhs_scale=q_op[u][2][rows, c : c + QB],
+                        start=True,
+                        stop=True,
+                    )
+                    at += QB
+
+        def exps(n):
+            h, g, parts = jobs[n]
+            at = 0
+            for j, q0, width in parts:
+                nc.scalar.activation(out=p_sb[h, g][:, j, q0 : q0 + width], in_=banks[n][:, at : at + width], func=ACT.Exp, bias=kb_sb[:, g, j : j + 1])
+                at += width
+            scores(n + 3)
+
+        def weights(h, g, q0, q1):
+            dst = w_op[h, g][0][:, PACK * q0 : PACK * q1].rearrange("p (c i j) -> p c j i", i=4, j=PACK)
+            nc.vector.tensor_tensor(
+                out=dst,
+                in0=p_sb[h, g][:, :, q0:q1].rearrange("p j (c i) -> p c j i", i=4),
+                in1=mt[g][:, :, q0:q1].rearrange("p j (c i) -> p c j i", i=4),
+                op=ALU.mult,
+            )
+
+        y_banks = {}
+
+        def values(h, b0, b1):
+            y = y_pool.tile([P, NQ // QB, E], F32, name="y")
+            y_banks[h, b0] = y
+            for b in range(b0, b1):
+                for g in range(PASSES):
+                    nc.tensor.matmul_mx(
+                        out=y[:, b - b0, :],
+                        lhsT=w_op[h, g][1][:, b * QB : (b + 1) * QB].bitcast(FP8X4),
+                        lhsT_scale=w_op[h, g][2][:, b * QB : (b + 1) * QB],
+                        rhs=v_op[h][1][:, g * E : (g + 1) * E].bitcast(FP8X4),
+                        rhs_scale=v_op[h][2][:, g * E : (g + 1) * E],
+                        start=(g == 0),
+                        stop=(g == PASSES - 1),
+                    )
+
+        def denominators(h, b0, b1):
+            cols = slice(4 * h + b0, 4 * h + b1)
+            nc.vector.tensor_tensor(out=den[:, cols], in0=y_banks[h, b0][:, 0 : b1 - b0, E - 1], in1=sink_sb[:, cols], op=ALU.add)
+
+        def inverses(h, b0, b1):
+            cols = slice(4 * h + b0, 4 * h + b1)
+            nc.vector.reciprocal(out=inv[:, cols], in_=den[:, cols])
+
+        def finish(h, b0, b1):
+            result = sb("out%d_%d" % (h, b0), [P, b1 - b0, E], F32)
+            for b in range(b0, b1):
+                nc.scalar.activation(out=result[:, b - b0, :], in_=y_banks[h, b0][:, b - b0, :], func=ACT.Copy, scale=inv[:, 4 * h + b : 4 * h + b + 1])
+            nc.sync.dma_start(out=out[h, b0 * QB : b1 * QB, :].rearrange("(b p) e -> p b e", p=P), in_=result[:])
+
+        round_k(0, "vector", 0, K_SPLIT)
+        round_k(0, "scalar", K_SPLIT, P)
+        quantise(k_op[0], 0, PASS)
+        for u in range(2):
+            round_q(u, "vector", 0, Q_SPLIT)
+            round_q(u, "scalar", Q_SPLIT, HALF // 4)
+        quantise(q_op[0], 0, HALF)
+        scores(0)
+        scores(1)
+        quantise(q_op[1], 0, HALF)
+        scores(2)
+        for j in range(PACK):
+            mask_times_t(0, j, "vector")
+        exps(0)
+        exps(1)
+        weights(0, 0, 0, HALF)
+        exps(2)
+        exps(3)
+        weights(0, 0, HALF, NQ)
+        quantise(w_op[0, 0], 0, HALF)
+        exps(4)
+        round_k(1, "vector", 0, 64)
+        quantise(w_op[0, 0], HALF, NQ)
+        round_k(1, "scalar", 64, P)
+        quantise(k_op[1], 0, PASS)
+        exps(5)
+        exps(6)
+        exps(7)
+        weights(1, 0, 0, HALF)
+        weights(1, 0, HALF, NQ)
+        quantise(w_op[1, 0], 0, HALF)
+        mask_times_t(1, 0, "vector")
+        mask_times_t(1, 1, "vector")
+        quantise(w_op[1, 0], HALF, NQ)
+        for n in range(8, 12):
+            exps(n)
+        mask_times_t(1, 2, "vector")
+        mask_times_t(1, 3, "vector")
+        weights(0, 1, 0, HALF)
+        weights(0, 1, HALF, NQ)
+        quantise(w_op[0, 1], 0, HALF)
+        exps(12)
+        exps(13)
+        round_v(0)
+        exps(14)
+        exps(15)
+        round_v(1)
+        quantise(v_op[0], 0, PASSES * E)
+        quantise(w_op[0, 1], HALF, NQ)
+        values(0, 0, 4)
+        weights(1, 1, 0, HALF)
+        quantise(v_op[1], 0, PASSES * E)
+        denominators(0, 0, 4)
+        quantise(w_op[1, 1], 0, HALF)
+        inverses(0, 0, 4)
+        values(1, 0, 2)
+        weights(1, 1, HALF, HALF + QB)
+        finish(0, 0, 4)
+        weights(1, 1, HALF + QB, NQ)
+        quantise(w_op[1, 1], HALF, HALF + QB)
+        denominators(1, 0, 2)
+        values(1, 2, 3)
+        quantise(w_op[1, 1], HALF + QB, NQ)
+        inverses(1, 0, 2)
+        finish(1, 0, 2)
+        values(1, 3, 4)
+        denominators(1, 2, 3)
+        inverses(1, 2, 3)
+        denominators(1, 3, 4)
+        finish(1, 2, 3)
+        inverses(1, 3, 4)
+        finish(1, 3, 4)

@@ -28,8 +28,8 @@ def tile_rows_a_exp_kb_mask_sink_kernel(tc, qT, kT, t, v, kb, mask, sink, out):
     nc = tc.nc
     with ExitStack() as ctx:
         keep = ctx.enter_context(tc.tile_pool(name="keep", bufs=1))
-        score_pools = [ctx.enter_context(tc.psum_pool(name="scores%d" % h, bufs=3)) for h in range(H)]
-        y_pool = ctx.enter_context(tc.psum_pool(name="y", bufs=2))
+        score_pools = [ctx.enter_context(tc.psum_pool(name="scores%d" % h, bufs=2)) for h in range(H)]
+        y_pool = ctx.enter_context(tc.psum_pool(name="y", bufs=4))
         ctx.enter_context(tc.manual_schedule())
 
         def sb(name, shape, dtype):
@@ -48,15 +48,15 @@ def tile_rows_a_exp_kb_mask_sink_kernel(tc, qT, kT, t, v, kb, mask, sink, out):
         t_sb = sb("t_sb", [P, PASSES, PACK], F32)
         sink_sb = sb("sink_sb", [P, H * NQ // QB], F32)
         k_raw = [sb("k_raw%d" % g, [P, PACK, PASS], F32) for g in range(PASSES)]
-        q_raw = sb("q_raw", [P, PACK, NQ], F32)
+        q_raw = [sb("q_raw%d" % u, [P, PACK, HALF], F32) for u in range(2)]
         mask_raw = [[sb("mask_raw%d_%d" % (g, u), [P, 2, NQ], F32) for u in range(2)] for g in range(PASSES)]
         v_raw = [sb("v_raw%d" % h, [P, PASSES, PACK, E], F32) for h in range(H)]
         mt = [sb("mt%d" % g, [P, PACK, NQ], F32) for g in range(PASSES)]
         k_op = [operand("k%d" % g, PASS) for g in range(PASSES)]
         q_op = [operand("q%d" % u, HALF) for u in range(2)]
         v_op = [operand("v%d" % h, PASSES * E) for h in range(H)]
-        w_op = {(h, g): operand("w%d_%d" % (h, g), NQ) for h in range(H) for g in range(PASSES)}
-        p_sb = {(h, g): sb("p%d_%d" % (h, g), [P, PACK, NQ], F32) for h in range(H) for g in range(PASSES)}
+        w_op = [operand("w%d" % n, HALF) for n in range(8)]
+        p_sb = [sb("p%d" % n, [P, PACK, HALF], F32) for n in range(8)]
         den = sb("den", [P, H * NQ // QB], F32)
         inv = sb("inv", [P, H * NQ // QB], F32)
 
@@ -66,8 +66,10 @@ def tile_rows_a_exp_kb_mask_sink_kernel(tc, qT, kT, t, v, kb, mask, sink, out):
         nc.scalar.dma_start(out=kb_sb[:], in_=kb.rearrange("(g p j) o -> p g (j o)", g=PASSES, j=PACK))
         nc.scalar.dma_start(out=t_sb[:], in_=t.rearrange("(g p j) o -> p g (j o)", g=PASSES, j=PACK))
         nc.scalar.activation(out=warm_out[:], in_=warm_in[:], func=ACT.Exp)
+        q_rows = qT.rearrange("h (p j) n -> (h p) j n", j=PACK)
+        nc.sync.dma_start(out=q_raw[0][:], in_=q_rows[:, :, 0:HALF])
         nc.sync.dma_start(out=k_raw[0][:], in_=k_rows[:, :, 0:PASS])
-        nc.sync.dma_start(out=q_raw[:], in_=qT.rearrange("h (p j) n -> (h p) j n", j=PACK))
+        nc.sync.dma_start(out=q_raw[1][:], in_=q_rows[:, :, HALF:NQ])
         for u in range(2):
             nc.sync.dma_start(out=mask_raw[0][u][:], in_=mask_rows[0, :, 2 * u : 2 * u + 2, :])
         nc.sync.dma_start(out=k_raw[1][:], in_=k_rows[:, :, PASS:N])
@@ -91,7 +93,7 @@ def tile_rows_a_exp_kb_mask_sink_kernel(tc, qT, kT, t, v, kb, mask, sink, out):
 
         def round_q(u, engine, c0, c1):
             dst = q_op[u][0][:].rearrange("p (c i j) -> p c j i", i=4, j=PACK)
-            src = q_raw[:, :, u * HALF : (u + 1) * HALF].rearrange("p j (c i) -> p c j i", i=4)
+            src = q_raw[u][:].rearrange("p j (c i) -> p c j i", i=4)
             copy_on(engine, dst[:, c0:c1], src[:, c0:c1])
 
         def round_v(h):
@@ -105,154 +107,155 @@ def tile_rows_a_exp_kb_mask_sink_kernel(tc, qT, kT, t, v, kb, mask, sink, out):
             else:
                 nc.scalar.activation(out=mt[g][:, j, :], in_=mask_raw[g][j // 2][:, j % 2, :], func=ACT.Copy, scale=t_sb[:, g, j : j + 1])
 
-        jobs = []
-        for u in range(2):
-            for j0 in (0, 2):
-                jobs.append((0, 0, [(j0, u * HALF, HALF), (j0 + 1, u * HALF, HALF)]))
-        for h, g in ((1, 0), (0, 1), (1, 1)):
-            for j in range(PACK):
-                jobs.append((h, g, [(j, 0, NQ)]))
+        units = [(g, u, h) for g in range(PASSES) for u in range(2) for h in range(H)]
         banks = {}
 
         def scores(n):
-            if n >= len(jobs):
-                return
-            h, g, parts = jobs[n]
-            bank = score_pools[h].tile([P, NQ], F32, name="bank")
-            banks[n] = bank
+            g, u, h = units[n]
             rows = slice(h * ROWS, (h + 1) * ROWS)
-            at = 0
-            for j, q0, width in parts:
-                for q in range(q0, q0 + width, QB):
-                    u, c = divmod(q, HALF)
-                    nc.tensor.matmul_mx(
-                        out=bank[:, at : at + QB],
-                        lhsT=k_op[g][1][rows, j * P : (j + 1) * P].bitcast(FP8X4),
-                        lhsT_scale=k_op[g][2][rows, j * P : (j + 1) * P],
-                        rhs=q_op[u][1][rows, c : c + QB].bitcast(FP8X4),
-                        rhs_scale=q_op[u][2][rows, c : c + QB],
-                        start=True,
-                        stop=True,
-                    )
-                    at += QB
+            for j0 in (0, 2):
+                bank = score_pools[h].tile([P, 2, HALF], F32, name="bank")
+                banks[n, j0] = bank
+                for j in (j0, j0 + 1):
+                    for c in range(0, HALF, QB):
+                        nc.tensor.matmul_mx(
+                            out=bank[:, j - j0, c : c + QB],
+                            lhsT=k_op[g][1][rows, j * P : (j + 1) * P].bitcast(FP8X4),
+                            lhsT_scale=k_op[g][2][rows, j * P : (j + 1) * P],
+                            rhs=q_op[u][1][rows, c : c + QB].bitcast(FP8X4),
+                            rhs_scale=q_op[u][2][rows, c : c + QB],
+                            start=True,
+                            stop=True,
+                        )
 
         def exps(n):
-            h, g, parts = jobs[n]
-            at = 0
-            for j, q0, width in parts:
-                nc.scalar.activation(out=p_sb[h, g][:, j, q0 : q0 + width], in_=banks[n][:, at : at + width], func=ACT.Exp, bias=kb_sb[:, g, j : j + 1])
-                at += width
-            scores(n + 3)
+            g, u, h = units[n]
+            for j in range(PACK):
+                nc.scalar.activation(out=p_sb[n][:, j, :], in_=banks[n, j // 2 * 2][:, j % 2, :], func=ACT.Exp, bias=kb_sb[:, g, j : j + 1])
 
-        def weights(h, g, q0, q1):
-            dst = w_op[h, g][0][:, PACK * q0 : PACK * q1].rearrange("p (c i j) -> p c j i", i=4, j=PACK)
+        def weights(n, q0=0, q1=HALF):
+            g, u, h = units[n]
+            dst = w_op[n][0][:, PACK * q0 : PACK * q1].rearrange("p (c i j) -> p c j i", i=4, j=PACK)
             nc.vector.tensor_tensor(
                 out=dst,
-                in0=p_sb[h, g][:, :, q0:q1].rearrange("p j (c i) -> p c j i", i=4),
-                in1=mt[g][:, :, q0:q1].rearrange("p j (c i) -> p c j i", i=4),
+                in0=p_sb[n][:, :, q0:q1].rearrange("p j (c i) -> p c j i", i=4),
+                in1=mt[g][:, :, u * HALF + q0 : u * HALF + q1].rearrange("p j (c i) -> p c j i", i=4),
                 op=ALU.mult,
             )
 
+        def quantise_w(n, q0=0, q1=HALF):
+            quantise(w_op[n], q0, q1)
+
         y_banks = {}
 
-        def values(h, b0, b1):
+        def col(n, b):
+            g, u, h = units[n]
+            return 4 * h + 2 * u + b
+
+        def values(n, b0=0, b1=2):
+            g, u, h = units[n]
             y = y_pool.tile([P, NQ // QB, E], F32, name="y")
-            y_banks[h, b0] = y
+            y_banks[n, b0] = y
             for b in range(b0, b1):
-                for g in range(PASSES):
+                for g, m in enumerate((n - 4, n)):
                     nc.tensor.matmul_mx(
                         out=y[:, b - b0, :],
-                        lhsT=w_op[h, g][1][:, b * QB : (b + 1) * QB].bitcast(FP8X4),
-                        lhsT_scale=w_op[h, g][2][:, b * QB : (b + 1) * QB],
+                        lhsT=w_op[m][1][:, b * QB : (b + 1) * QB].bitcast(FP8X4),
+                        lhsT_scale=w_op[m][2][:, b * QB : (b + 1) * QB],
                         rhs=v_op[h][1][:, g * E : (g + 1) * E].bitcast(FP8X4),
                         rhs_scale=v_op[h][2][:, g * E : (g + 1) * E],
                         start=(g == 0),
                         stop=(g == PASSES - 1),
                     )
 
-        def denominators(h, b0, b1):
-            cols = slice(4 * h + b0, 4 * h + b1)
-            nc.vector.tensor_tensor(out=den[:, cols], in0=y_banks[h, b0][:, 0 : b1 - b0, E - 1], in1=sink_sb[:, cols], op=ALU.add)
+        def denominators(n, b0=0, b1=2):
+            cols = slice(col(n, b0), col(n, b1))
+            nc.vector.tensor_tensor(out=den[:, cols], in0=y_banks[n, b0][:, 0 : b1 - b0, E - 1], in1=sink_sb[:, cols], op=ALU.add)
 
-        def inverses(h, b0, b1):
-            cols = slice(4 * h + b0, 4 * h + b1)
+        def inverses(n, b0=0, b1=2):
+            cols = slice(col(n, b0), col(n, b1))
             nc.vector.reciprocal(out=inv[:, cols], in_=den[:, cols])
 
-        def finish(h, b0, b1):
-            result = sb("out%d_%d" % (h, b0), [P, b1 - b0, E], F32)
+        def finish(n, b0=0, b1=2):
+            g, u, h = units[n]
+            result = sb("out%d_%d" % (n, b0), [P, b1 - b0, E], F32)
             for b in range(b0, b1):
-                nc.scalar.activation(out=result[:, b - b0, :], in_=y_banks[h, b0][:, b - b0, :], func=ACT.Copy, scale=inv[:, 4 * h + b : 4 * h + b + 1])
-            nc.sync.dma_start(out=out[h, b0 * QB : b1 * QB, :].rearrange("(b p) e -> p b e", p=P), in_=result[:])
+                nc.scalar.activation(out=result[:, b - b0, :], in_=y_banks[n, b0][:, b - b0, :], func=ACT.Copy, scale=inv[:, col(n, b) : col(n, b) + 1])
+            nc.sync.dma_start(out=out[h, u * HALF + b0 * QB : u * HALF + b1 * QB, :].rearrange("(b p) e -> p b e", p=P), in_=result[:])
 
+        round_q(0, "vector", 0, Q_SPLIT)
+        round_q(0, "scalar", Q_SPLIT, HALF // 4)
+        quantise(q_op[0], 0, HALF)
         round_k(0, "vector", 0, K_SPLIT)
         round_k(0, "scalar", K_SPLIT, P)
-        quantise(k_op[0], 0, PASS)
-        for u in range(2):
-            round_q(u, "vector", 0, Q_SPLIT)
-            round_q(u, "scalar", Q_SPLIT, HALF // 4)
-        quantise(q_op[0], 0, HALF)
+        quantise(k_op[0], 0, PASS // 2)
+        quantise(k_op[0], PASS // 2, PASS)
         scores(0)
         scores(1)
+        round_q(1, "vector", 0, HALF // 4)
+        mask_times_t(0, 0, "vector")
         quantise(q_op[1], 0, HALF)
-        scores(2)
-        for j in range(PACK):
+        for j in range(1, PACK):
             mask_times_t(0, j, "vector")
         exps(0)
+        scores(2)
+        weights(0)
         exps(1)
-        weights(0, 0, 0, HALF)
+        scores(3)
+        weights(1)
+        quantise_w(0)
+        round_k(1, "vector", 0, P)
+        quantise_w(1)
         exps(2)
+        quantise(k_op[1], 0, PASS // 2)
+        quantise(k_op[1], PASS // 2, PASS)
+        scores(4)
         exps(3)
-        weights(0, 0, HALF, NQ)
-        quantise(w_op[0, 0], 0, HALF)
-        exps(4)
-        round_k(1, "vector", 0, 64)
-        quantise(w_op[0, 0], HALF, NQ)
-        round_k(1, "scalar", 64, P)
-        quantise(k_op[1], 0, PASS)
-        exps(5)
-        exps(6)
-        exps(7)
-        weights(1, 0, 0, HALF)
-        weights(1, 0, HALF, NQ)
-        quantise(w_op[1, 0], 0, HALF)
-        mask_times_t(1, 0, "vector")
-        mask_times_t(1, 1, "vector")
-        quantise(w_op[1, 0], HALF, NQ)
-        for n in range(8, 12):
-            exps(n)
-        mask_times_t(1, 2, "vector")
+        scores(5)
+        weights(2)
+        weights(3)
+        quantise_w(2)
+        for j in range(3):
+            mask_times_t(1, j, "scalar")
         mask_times_t(1, 3, "vector")
-        weights(0, 1, 0, HALF)
-        weights(0, 1, HALF, NQ)
-        quantise(w_op[0, 1], 0, HALF)
-        exps(12)
-        exps(13)
+        quantise_w(3)
+        exps(4)
+        scores(6)
+        weights(4)
         round_v(0)
-        exps(14)
-        exps(15)
-        round_v(1)
+        exps(5)
+        scores(7)
+        weights(5)
+        quantise_w(4)
         quantise(v_op[0], 0, PASSES * E)
-        quantise(w_op[0, 1], HALF, NQ)
-        values(0, 0, 4)
-        weights(1, 1, 0, HALF)
+        values(4)
+        quantise_w(5)
+        exps(6)
+        round_v(1)
+        weights(6)
+        denominators(4)
         quantise(v_op[1], 0, PASSES * E)
-        denominators(0, 0, 4)
-        quantise(w_op[1, 1], 0, HALF)
-        inverses(0, 0, 4)
-        values(1, 0, 2)
-        weights(1, 1, HALF, HALF + QB)
-        finish(0, 0, 4)
-        weights(1, 1, HALF + QB, NQ)
-        quantise(w_op[1, 1], HALF, HALF + QB)
-        denominators(1, 0, 2)
-        values(1, 2, 3)
-        quantise(w_op[1, 1], HALF + QB, NQ)
-        inverses(1, 0, 2)
-        finish(1, 0, 2)
-        values(1, 3, 4)
-        denominators(1, 2, 3)
-        inverses(1, 2, 3)
-        denominators(1, 3, 4)
-        finish(1, 2, 3)
-        inverses(1, 3, 4)
-        finish(1, 3, 4)
+        values(5)
+        inverses(4)
+        exps(7)
+        finish(4)
+        quantise_w(6)
+        values(6)
+        weights(7, 0, QB)
+        denominators(5)
+        weights(7, QB, HALF)
+        inverses(5)
+        quantise_w(7, 0, QB)
+        values(7, 0, 1)
+        denominators(6)
+        quantise_w(7, QB, HALF)
+        finish(5)
+        values(7, 1, 2)
+        inverses(6)
+        finish(6)
+        denominators(7, 0, 1)
+        denominators(7, 1, 2)
+        inverses(7, 0, 1)
+        inverses(7, 1, 2)
+        finish(7, 0, 1)
+        finish(7, 1, 2)

@@ -21,7 +21,7 @@ ROWS = D // PACK
 QB = 128
 HALF = NQ // 2
 K_SPLIT = 84
-Q_SPLIT = 42
+Q_SPLIT = 32
 
 
 def tile_rows_a_exp_kb_mask_sink_kernel(tc, qT, kT, t, v, kb, mask, sink, out):
@@ -42,14 +42,14 @@ def tile_rows_a_exp_kb_mask_sink_kernel(tc, qT, kT, t, v, kb, mask, sink, out):
             values, codes, scales = op
             nc.vector.quantize_mx(out=codes[:, c0:c1].bitcast(FP8X4), scales=scales[:, c0:c1], in_=values[:, PACK * c0 : PACK * c1])
 
-        warm_in = sb("warm_in", [P, 1], F32)
-        warm_out = sb("warm_out", [P, 1], F32)
         kb_sb = sb("kb_sb", [P, PASSES, PACK], F32)
         t_sb = sb("t_sb", [P, PASSES, PACK], F32)
         sink_sb = sb("sink_sb", [P, H * NQ // QB], F32)
         k_raw = [sb("k_raw%d" % g, [P, PACK, PASS], F32) for g in range(PASSES)]
         q_raw = [sb("q_raw%d" % u, [P, PACK, HALF], F32) for u in range(2)]
-        mask_raw = [[sb("mask_raw%d_%d" % (g, u), [P, 2, NQ], F32) for u in range(2)] for g in range(PASSES)]
+        mask_pieces = [((0, 2), (2, 3), (3, 4)), ((0, 2), (2, 4))]
+        mask_raw = [[sb("mask_raw%d_%d" % (g, j0), [P, j1 - j0, NQ], F32) for j0, j1 in mask_pieces[g]] for g in range(PASSES)]
+        mask_slot = {(g, j): mask_raw[g][n][:, j - j0, :] for g in range(PASSES) for n, (j0, j1) in enumerate(mask_pieces[g]) for j in range(j0, j1)}
         v_raw = [sb("v_raw%d" % h, [P, PASSES, PACK, E], F32) for h in range(H)]
         mt = [sb("mt%d" % g, [P, PACK, NQ], F32) for g in range(PASSES)]
         k_op = [operand("k%d" % g, PASS) for g in range(PASSES)]
@@ -62,19 +62,17 @@ def tile_rows_a_exp_kb_mask_sink_kernel(tc, qT, kT, t, v, kb, mask, sink, out):
 
         k_rows = kT.rearrange("h (p j) n -> (h p) j n", j=PACK)
         mask_rows = mask.rearrange("(g p j) q -> g p j q", g=PASSES, j=PACK)
-        nc.vector.memset(warm_in[:], 0.0)
         nc.scalar.dma_start(out=kb_sb[:], in_=kb.rearrange("(g p j) o -> p g (j o)", g=PASSES, j=PACK))
         nc.scalar.dma_start(out=t_sb[:], in_=t.rearrange("(g p j) o -> p g (j o)", g=PASSES, j=PACK))
-        nc.scalar.activation(out=warm_out[:], in_=warm_in[:], func=ACT.Exp)
         q_rows = qT.rearrange("h (p j) n -> (h p) j n", j=PACK)
-        nc.sync.dma_start(out=q_raw[0][:], in_=q_rows[:, :, 0:HALF])
         nc.sync.dma_start(out=k_raw[0][:], in_=k_rows[:, :, 0:PASS])
+        nc.sync.dma_start(out=q_raw[0][:], in_=q_rows[:, :, 0:HALF])
         nc.sync.dma_start(out=q_raw[1][:], in_=q_rows[:, :, HALF:NQ])
-        for u in range(2):
-            nc.sync.dma_start(out=mask_raw[0][u][:], in_=mask_rows[0, :, 2 * u : 2 * u + 2, :])
+        for n, (j0, j1) in enumerate(mask_pieces[0]):
+            nc.sync.dma_start(out=mask_raw[0][n][:], in_=mask_rows[0, :, j0:j1, :])
         nc.sync.dma_start(out=k_raw[1][:], in_=k_rows[:, :, PASS:N])
-        for u in range(2):
-            nc.sync.dma_start(out=mask_raw[1][u][:], in_=mask_rows[1, :, 2 * u : 2 * u + 2, :])
+        for n, (j0, j1) in enumerate(mask_pieces[1]):
+            nc.sync.dma_start(out=mask_raw[1][n][:], in_=mask_rows[1, :, j0:j1, :])
         for h in range(H):
             nc.sync.dma_start(out=v_raw[h][:].rearrange("p g j e -> p g (j e)"), in_=v[h].rearrange("(g p j) e -> p g (j e)", g=PASSES, j=PACK))
         with nc.allow_non_contiguous_dma(reason="one sink value a partition"):
@@ -84,7 +82,7 @@ def tile_rows_a_exp_kb_mask_sink_kernel(tc, qT, kT, t, v, kb, mask, sink, out):
             if engine == "vector":
                 nc.vector.tensor_copy(out=dst, in_=src)
             else:
-                nc.scalar.copy(out=dst, in_=src)
+                nc.scalar.activation(out=dst, in_=src, func=ACT.Copy)
 
         def round_k(g, engine, s0, s1):
             dst = k_op[g][0][:].rearrange("p (r s j) -> p s j r", r=PACK, j=PACK)
@@ -103,9 +101,9 @@ def tile_rows_a_exp_kb_mask_sink_kernel(tc, qT, kT, t, v, kb, mask, sink, out):
 
         def mask_times_t(g, j, engine):
             if engine == "vector":
-                nc.vector.tensor_scalar(out=mt[g][:, j, :], in0=mask_raw[g][j // 2][:, j % 2, :], scalar1=t_sb[:, g, j : j + 1], scalar2=None, op0=ALU.mult)
+                nc.vector.tensor_scalar(out=mt[g][:, j, :], in0=mask_slot[g, j], scalar1=t_sb[:, g, j : j + 1], scalar2=None, op0=ALU.mult)
             else:
-                nc.scalar.activation(out=mt[g][:, j, :], in_=mask_raw[g][j // 2][:, j % 2, :], func=ACT.Copy, scale=t_sb[:, g, j : j + 1])
+                nc.scalar.activation(out=mt[g][:, j, :], in_=mask_slot[g, j], func=ACT.Copy, scale=t_sb[:, g, j : j + 1])
 
         units = [(g, u, h) for g in range(PASSES) for u in range(2) for h in range(H)]
         banks = {}
@@ -183,19 +181,18 @@ def tile_rows_a_exp_kb_mask_sink_kernel(tc, qT, kT, t, v, kb, mask, sink, out):
                 nc.scalar.activation(out=result[:, b - b0, :], in_=y_banks[n, b0][:, b - b0, :], func=ACT.Copy, scale=inv[:, col(n, b) : col(n, b) + 1])
             nc.sync.dma_start(out=out[h, u * HALF + b0 * QB : u * HALF + b1 * QB, :].rearrange("(b p) e -> p b e", p=P), in_=result[:])
 
-        round_q(0, "vector", 0, Q_SPLIT)
-        round_q(0, "scalar", Q_SPLIT, HALF // 4)
-        quantise(q_op[0], 0, HALF)
         round_k(0, "vector", 0, K_SPLIT)
         round_k(0, "scalar", K_SPLIT, P)
         quantise(k_op[0], 0, PASS // 2)
+        round_q(0, "vector", 0, Q_SPLIT)
+        round_q(0, "scalar", Q_SPLIT, HALF // 4)
         quantise(k_op[0], PASS // 2, PASS)
+        quantise(q_op[0], 0, HALF)
         scores(0)
         scores(1)
         round_q(1, "vector", 0, HALF // 4)
-        mask_times_t(0, 0, "vector")
         quantise(q_op[1], 0, HALF)
-        for j in range(1, PACK):
+        for j in range(PACK):
             mask_times_t(0, j, "vector")
         exps(0)
         scores(2)
@@ -215,15 +212,14 @@ def tile_rows_a_exp_kb_mask_sink_kernel(tc, qT, kT, t, v, kb, mask, sink, out):
         weights(2)
         weights(3)
         quantise_w(2)
-        for j in range(3):
+        for j in range(PACK):
             mask_times_t(1, j, "scalar")
-        mask_times_t(1, 3, "vector")
         quantise_w(3)
         exps(4)
         scores(6)
         weights(4)
-        round_v(0)
         exps(5)
+        round_v(0)
         scores(7)
         weights(5)
         quantise_w(4)

from contextlib import ExitStack

import concourse.mybir as mybir

H, D, NQ, N, E = 2, 256, 512, 1024, 128
FLOPS = 2 * H * NQ * N * (D + E)

F32 = mybir.dt.float32
BF16 = mybir.dt.bfloat16
U32 = mybir.dt.uint32
U8 = mybir.dt.uint8
FP8X4 = mybir.dt.float8_e4m3fn_x4
ACT = mybir.ActivationFunctionType
ALU = mybir.AluOpType

P = 128
PACK = 4
PASS = P * PACK
PASSES = N // PASS
ROWS = D // PACK
QB = 128
HALF = NQ // 2
K_SPLIT = 84
Q_SPLIT = 32


def tile_rows_a_exp_kb_mask_sink_kernel(tc, qT, kT, t, v, kb, mask, sink, out):
    nc = tc.nc
    with ExitStack() as ctx:
        keep = ctx.enter_context(tc.tile_pool(name="keep", bufs=1))
        score_pools = [ctx.enter_context(tc.psum_pool(name="scores%d" % h, bufs=2)) for h in range(H)]
        y_pool = ctx.enter_context(tc.psum_pool(name="y", bufs=4))
        ctx.enter_context(tc.manual_schedule())

        def sb(name, shape, dtype):
            return keep.tile(shape, dtype, name=name, align_bytes=64)

        def operand(name, words):
            return (sb(name + "_bf", [P, PACK * words], BF16), sb(name + "_codes", [P, words], U32), sb(name + "_scales", [P, words], U8))

        def quantise(op, c0, c1):
            values, codes, scales = op
            nc.vector.quantize_mx(out=codes[:, c0:c1].bitcast(FP8X4), scales=scales[:, c0:c1], in_=values[:, PACK * c0 : PACK * c1])

        kb_sb = sb("kb_sb", [P, PASSES, PACK], F32)
        t_sb = sb("t_sb", [P, PASSES, PACK], F32)
        sink_sb = sb("sink_sb", [P, H * NQ // QB], F32)
        k_raw = [sb("k_raw%d" % g, [P, PACK, PASS], F32) for g in range(PASSES)]
        q_raw = [sb("q_raw%d" % u, [P, PACK, HALF], F32) for u in range(2)]
        mask_pieces = [((0, 2), (2, 3), (3, 4)), ((0, 2), (2, 4))]
        mask_raw = [[sb("mask_raw%d_%d" % (g, j0), [P, j1 - j0, NQ], F32) for j0, j1 in mask_pieces[g]] for g in range(PASSES)]
        mask_slot = {(g, j): mask_raw[g][n][:, j - j0, :] for g in range(PASSES) for n, (j0, j1) in enumerate(mask_pieces[g]) for j in range(j0, j1)}
        v_raw = [sb("v_raw%d" % h, [P, PASSES, PACK, E], F32) for h in range(H)]
        mt = [sb("mt%d" % g, [P, PACK, NQ], F32) for g in range(PASSES)]
        k_op = [operand("k%d" % g, PASS) for g in range(PASSES)]
        q_op = [operand("q%d" % u, HALF) for u in range(2)]
        v_op = [operand("v%d" % h, PASSES * E) for h in range(H)]
        w_op = [operand("w%d" % n, HALF) for n in range(8)]
        p_sb = [sb("p%d" % n, [P, PACK, HALF], F32) for n in range(8)]
        den = sb("den", [P, H * NQ // QB], F32)
        inv = sb("inv", [P, H * NQ // QB], F32)

        k_rows = kT.rearrange("h (p j) n -> (h p) j n", j=PACK)
        mask_rows = mask.rearrange("(g p j) q -> g p j q", g=PASSES, j=PACK)
        nc.scalar.dma_start(out=kb_sb[:], in_=kb.rearrange("(g p j) o -> p g (j o)", g=PASSES, j=PACK))
        nc.scalar.dma_start(out=t_sb[:], in_=t.rearrange("(g p j) o -> p g (j o)", g=PASSES, j=PACK))
        q_rows = qT.rearrange("h (p j) n -> (h p) j n", j=PACK)
        nc.sync.dma_start(out=k_raw[0][:], in_=k_rows[:, :, 0:PASS])
        nc.sync.dma_start(out=q_raw[0][:], in_=q_rows[:, :, 0:HALF])
        nc.sync.dma_start(out=q_raw[1][:], in_=q_rows[:, :, HALF:NQ])
        for n, (j0, j1) in enumerate(mask_pieces[0]):
            nc.sync.dma_start(out=mask_raw[0][n][:], in_=mask_rows[0, :, j0:j1, :])
        nc.sync.dma_start(out=k_raw[1][:], in_=k_rows[:, :, PASS:N])
        for n, (j0, j1) in enumerate(mask_pieces[1]):
            nc.sync.dma_start(out=mask_raw[1][n][:], in_=mask_rows[1, :, j0:j1, :])
        for h in range(H):
            nc.sync.dma_start(out=v_raw[h][:].rearrange("p g j e -> p g (j e)"), in_=v[h].rearrange("(g p j) e -> p g (j e)", g=PASSES, j=PACK))
        with nc.allow_non_contiguous_dma(reason="one sink value a partition"):
            nc.sync.dma_start(out=sink_sb[:].unsqueeze(2), in_=sink.rearrange("h (b p) o -> p (h b) o", p=P))

        def copy_on(engine, dst, src):
            if engine == "vector":
                nc.vector.tensor_copy(out=dst, in_=src)
            else:
                nc.scalar.activation(out=dst, in_=src, func=ACT.Copy)

        def round_k(g, engine, s0, s1):
            dst = k_op[g][0][:].rearrange("p (r s j) -> p s j r", r=PACK, j=PACK)
            src = k_raw[g][:].rearrange("p j (s r) -> p s j r", r=PACK)
            copy_on(engine, dst[:, s0:s1], src[:, s0:s1])

        def round_q(u, engine, c0, c1):
            dst = q_op[u][0][:].rearrange("p (c i j) -> p c j i", i=4, j=PACK)
            src = q_raw[u][:].rearrange("p j (c i) -> p c j i", i=4)
            copy_on(engine, dst[:, c0:c1], src[:, c0:c1])

        def round_v(h):
            dst = v_op[h][0][:].rearrange("p (g c i j) -> p g c j i", g=PASSES, i=4, j=PACK)
            src = v_raw[h][:].rearrange("p g j (c i) -> p g c j i", i=4)
            nc.scalar.copy(out=dst, in_=src)

        def mask_times_t(g, j, engine):
            if engine == "vector":
                nc.vector.tensor_scalar(out=mt[g][:, j, :], in0=mask_slot[g, j], scalar1=t_sb[:, g, j : j + 1], scalar2=None, op0=ALU.mult)
            else:
                nc.scalar.activation(out=mt[g][:, j, :], in_=mask_slot[g, j], func=ACT.Copy, scale=t_sb[:, g, j : j + 1])

        units = [(g, u, h) for g in range(PASSES) for u in range(2) for h in range(H)]
        banks = {}

        def scores(n):
            g, u, h = units[n]
            rows = slice(h * ROWS, (h + 1) * ROWS)
            for j0 in (0, 2):
                bank = score_pools[h].tile([P, 2, HALF], F32, name="bank")
                banks[n, j0] = bank
                for j in (j0, j0 + 1):
                    for c in range(0, HALF, QB):
                        nc.tensor.matmul_mx(
                            out=bank[:, j - j0, c : c + QB],
                            lhsT=k_op[g][1][rows, j * P : (j + 1) * P].bitcast(FP8X4),
                            lhsT_scale=k_op[g][2][rows, j * P : (j + 1) * P],
                            rhs=q_op[u][1][rows, c : c + QB].bitcast(FP8X4),
                            rhs_scale=q_op[u][2][rows, c : c + QB],
                            start=True,
                            stop=True,
                        )

        def exps(n):
            g, u, h = units[n]
            for j in range(PACK):
                nc.scalar.activation(out=p_sb[n][:, j, :], in_=banks[n, j // 2 * 2][:, j % 2, :], func=ACT.Exp, bias=kb_sb[:, g, j : j + 1])

        def weights(n, q0=0, q1=HALF):
            g, u, h = units[n]
            dst = w_op[n][0][:, PACK * q0 : PACK * q1].rearrange("p (c i j) -> p c j i", i=4, j=PACK)
            nc.vector.tensor_tensor(
                out=dst,
                in0=p_sb[n][:, :, q0:q1].rearrange("p j (c i) -> p c j i", i=4),
                in1=mt[g][:, :, u * HALF + q0 : u * HALF + q1].rearrange("p j (c i) -> p c j i", i=4),
                op=ALU.mult,
            )

        def quantise_w(n, q0=0, q1=HALF):
            quantise(w_op[n], q0, q1)

        y_banks = {}

        def col(n, b):
            g, u, h = units[n]
            return 4 * h + 2 * u + b

        def values(n, b0=0, b1=2):
            g, u, h = units[n]
            y = y_pool.tile([P, NQ // QB, E], F32, name="y")
            y_banks[n, b0] = y
            for b in range(b0, b1):
                for g, m in enumerate((n - 4, n)):
                    nc.tensor.matmul_mx(
                        out=y[:, b - b0, :],
                        lhsT=w_op[m][1][:, b * QB : (b + 1) * QB].bitcast(FP8X4),
                        lhsT_scale=w_op[m][2][:, b * QB : (b + 1) * QB],
                        rhs=v_op[h][1][:, g * E : (g + 1) * E].bitcast(FP8X4),
                        rhs_scale=v_op[h][2][:, g * E : (g + 1) * E],
                        start=(g == 0),
                        stop=(g == PASSES - 1),
                    )

        def denominators(n, b0=0, b1=2):
            cols = slice(col(n, b0), col(n, b1))
            nc.vector.tensor_tensor(out=den[:, cols], in0=y_banks[n, b0][:, 0 : b1 - b0, E - 1], in1=sink_sb[:, cols], op=ALU.add)

        def inverses(n, b0=0, b1=2):
            cols = slice(col(n, b0), col(n, b1))
            nc.vector.reciprocal(out=inv[:, cols], in_=den[:, cols])

        def finish(n, b0=0, b1=2):
            g, u, h = units[n]
            result = sb("out%d_%d" % (n, b0), [P, b1 - b0, E], F32)
            for b in range(b0, b1):
                nc.scalar.activation(out=result[:, b - b0, :], in_=y_banks[n, b0][:, b - b0, :], func=ACT.Copy, scale=inv[:, col(n, b) : col(n, b) + 1])
            nc.sync.dma_start(out=out[h, u * HALF + b0 * QB : u * HALF + b1 * QB, :].rearrange("(b p) e -> p b e", p=P), in_=result[:])

        round_k(0, "vector", 0, K_SPLIT)
        round_k(0, "scalar", K_SPLIT, P)
        quantise(k_op[0], 0, PASS // 2)
        round_q(0, "vector", 0, Q_SPLIT)
        round_q(0, "scalar", Q_SPLIT, HALF // 4)
        quantise(k_op[0], PASS // 2, PASS)
        quantise(q_op[0], 0, HALF)
        scores(0)
        scores(1)
        round_q(1, "vector", 0, HALF // 4)
        quantise(q_op[1], 0, HALF)
        for j in range(PACK):
            mask_times_t(0, j, "vector")
        exps(0)
        scores(2)
        weights(0)
        exps(1)
        scores(3)
        weights(1)
        quantise_w(0)
        round_k(1, "vector", 0, P)
        quantise_w(1)
        exps(2)
        quantise(k_op[1], 0, PASS // 2)
        quantise(k_op[1], PASS // 2, PASS)
        scores(4)
        exps(3)
        scores(5)
        weights(2)
        weights(3)
        quantise_w(2)
        for j in range(PACK):
            mask_times_t(1, j, "scalar")
        quantise_w(3)
        exps(4)
        scores(6)
        weights(4)
        exps(5)
        round_v(0)
        scores(7)
        weights(5)
        quantise_w(4)
        quantise(v_op[0], 0, PASSES * E)
        values(4)
        quantise_w(5)
        exps(6)
        round_v(1)
        weights(6)
        denominators(4)
        quantise(v_op[1], 0, PASSES * E)
        values(5)
        inverses(4)
        exps(7)
        finish(4)
        quantise_w(6)
        values(6)
        weights(7, 0, QB)
        denominators(5)
        weights(7, QB, HALF)
        inverses(5)
        quantise_w(7, 0, QB)
        values(7, 0, 1)
        denominators(6)
        quantise_w(7, QB, HALF)
        finish(5)
        values(7, 1, 2)
        inverses(6)
        finish(6)
        denominators(7, 0, 1)
        denominators(7, 1, 2)
        inverses(7, 0, 1)
        inverses(7, 1, 2)
        finish(7, 0, 1)
        finish(7, 1, 2)
